import numpy as np
import ml_dtypes


def mxq(x, axis, fmt="e4m3"):
    dtype, down = {"e4m3": (ml_dtypes.float8_e4m3fn, 7), "e5m2": (ml_dtypes.float8_e5m2, 14)}[fmt]
    v = np.moveaxis(np.asarray(x, np.float32).astype(ml_dtypes.bfloat16).astype(np.float64), axis, -1)
    blocks = v.reshape(v.shape[:-1] + (-1, 32))
    amax = np.abs(blocks).max(-1, keepdims=True)
    byte = np.maximum(np.where(amax > 0, np.frexp(amax)[1] - 1 + 127, 0) - down, 1)
    scale = np.exp2(byte - 127.0)
    codes = (blocks / scale).astype(np.float32).astype(dtype).astype(np.float64)
    return np.moveaxis((codes * scale).reshape(v.shape), -1, axis)


WIDE = False


def mx_kscale(k):
    if not WIDE:
        return np.ones(k)
    levels = np.array([10, -10, 5, -5, 0])
    if k % 512:
        return np.exp2(np.random.permutation(np.resize(levels, k // 32))).repeat(32)
    a = np.empty((k // 512, 16))
    for p in range(k // 512):
        a[p, :8] = np.random.permutation(np.resize(levels, 8))
        for g in range(8):
            far = levels[np.abs(levels - a[p, g]) >= 10]
            a[p, g + 8] = far[np.random.randint(len(far))]
    return np.exp2(a.ravel()).repeat(32)


def f64(x):
    return np.asarray(x).astype(np.float64)


def striped(idx):
    return np.tile(idx.reshape(-1, 16).T, (8, 1)).astype(np.uint16)


def unstriped(offs):
    return offs[:16].T.reshape(-1).astype(np.int64)


E2M1 = np.array([0.0, 0.5, 1.0, 1.5, 2.0, 3.0, 4.0, 6.0, -0.0, -0.5, -1.0, -1.5, -2.0, -3.0, -4.0, -6.0])


def pack_weight(w, fmt):
    k, n = w.shape
    w = f64(np.asarray(w, np.float32).astype(ml_dtypes.bfloat16)).reshape(k // 32, 32, n)
    amax = np.abs(w).max(1)
    if fmt == "e4m3":
        byte = np.frexp(amax)[1] - 1 + 127 - 7
    else:
        mant, ex = np.frexp(amax / 6.0)
        byte = np.where(mant > 0.5, ex, ex - 1) + 127
    byte = np.clip(np.where(amax > 0, byte, 1), 1, 254)
    scaled = (w * np.exp2(127.0 - byte)[:, None, :]).reshape(k, n).astype(np.float32)
    by_word = np.ascontiguousarray(scaled.reshape(k // 512, 128, 4, n).transpose(0, 1, 3, 2))
    if fmt == "e4m3":
        words = by_word.astype(ml_dtypes.float8_e4m3fn).view(np.uint8)
    else:
        c = by_word.astype(ml_dtypes.float4_e2m1fn).view(np.uint8) & 0xF
        words = (c[..., 0::2] | (c[..., 1::2] << 4)).reshape(k // 512, 128, 2 * n)
    return np.ascontiguousarray(words), np.ascontiguousarray(byte.astype(np.uint8).reshape(k // 512, 16, n))


def unpack_weight(words, scales, fmt):
    g, _, n = scales.shape
    words = np.ascontiguousarray(words).reshape(g, 128, n, -1)
    if fmt == "e4m3":
        vals = words.view(ml_dtypes.float8_e4m3fn).astype(np.float64)
    else:
        nib = np.empty((g, 128, n, 4), np.uint8)
        nib[..., 0::2] = words & 0xF
        nib[..., 1::2] = words >> 4
        vals = E2M1[nib]
    vals = vals * np.repeat(np.exp2(scales.astype(np.float64) - 127.0), 8, axis=1)[..., None]
    return vals.transpose(0, 1, 3, 2).reshape(g * 512, n)


def relu2(v):
    return np.maximum(v, 0.0) ** 2


K, T, E, C, N = 1536, 640, 2, 256, 512
K8 = 512


def by_expert(wq, xq):
    return np.concatenate([wq[e].T @ xq[:, e * C:(e + 1) * C] for e in range(E)], axis=1)


def setup_inputs():
    n = np.random.standard_normal
    s = mx_kscale(K)[:, None]
    w = n((E, K, N)) / np.sqrt(K) / s[None]
    w8 = [pack_weight(m[:K8], "e4m3") for m in w]
    w4 = [pack_weight(m[K8:], "e2m1") for m in w]
    return {
        "xT": (n((K, T)) * s).astype(np.float32),
        "xr": n((N, T)).astype(np.float32),
        "w8_words": np.stack([m[0] for m in w8]),
        "w8_scales": np.stack([m[1] for m in w8]),
        "w4_words": np.stack([m[0] for m in w4]),
        "w4_scales": np.stack([m[1] for m in w4]),
        "b": (0.3 * n((N, E))).astype(np.float32),
        "gate": np.tile(np.random.uniform(0.2, 1.0, E * C), (N, 1)).astype(np.float32),
        "offs": striped(np.random.permutation(T)[:E * C]),
    }


def reference(xT, xr, w8_words, w8_scales, w4_words, w4_scales, b, gate, offs):
    idx = unstriped(offs)
    w = np.stack([np.concatenate([unpack_weight(w8_words[e], w8_scales[e], "e4m3"), unpack_weight(w4_words[e], w4_scales[e], "e2m1")]) for e in range(E)])
    xq = mxq(f64(xT)[:, idx], 0, "e4m3")
    y = by_expert(w, xq)
    y = relu2(y + np.repeat(f64(b), C, axis=1))
    out = f64(xr).copy()
    out[:, idx] += f64(gate) * y
    return out

@@ -1,0 +1,210 @@
+from contextlib import ExitStack
+
+import concourse.mybir as mybir
+
+K, T, E, C, N = 1536, 640, 2, 256, 512
+S = E * C
+P = 128
+PASSES = 3
+NB = N // P
+HALF = 128
+
+FLOPS = 2 * K * N * S
+BYTES = 4 * K * T + 4 * N * T + E * (K // 3) * N + E * (2 * K // 3) * N // 2 + E * (K // 32) * N + 4 * N * E + 4 * S + 2 * P * (S // 16) + 4 * N * T
+
+F32 = mybir.dt.float32
+BF16 = mybir.dt.bfloat16
+I32 = mybir.dt.int32
+U32 = mybir.dt.uint32
+U16 = mybir.dt.uint16
+U8 = mybir.dt.uint8
+FP8X4 = mybir.dt.float8_e4m3fn_x4
+FP4X4 = mybir.dt.float4_e2m1fn_x4
+ACT = mybir.ActivationFunctionType
+ALU = mybir.AluOpType
+
+
+def tile_moe_res_lin_relu2_kernel(tc, xT, xr, w8_words, w8_scales, w4_words, w4_scales, b, gate, offs, out):
+    nc = tc.nc
+    with ExitStack() as ctx:
+        lists = ctx.enter_context(tc.tile_pool(name="lists", bufs=1))
+        hold = ctx.enter_context(tc.tile_pool(name="hold", bufs=1))
+        psum = ctx.enter_context(tc.psum_pool(name="psum", bufs=1))
+
+        offsets = lists.tile([P, S // 16], U16, name="offsets")
+        x_raw = [hold.tile([P, 4, T], F32, name=f"x_raw{a}", align_bytes=64) for a in range(PASSES)]
+        x_grp = [hold.tile([P, T, 4], BF16, name=f"x_grp{a}", align_bytes=64) for a in range(PASSES)]
+        words = [hold.tile([P, T], U32, name=f"words{a}", align_bytes=64) for a in range(PASSES)]
+        bytes01 = hold.tile([P, T], U8, name="scale_bytes01", align_bytes=64)
+        bytes2 = hold.tile([P, T], U8, name="scale_bytes2", align_bytes=64)
+        bytes_ = [bytes01[4:P, :], bytes01[:], bytes2[:]]
+        g_words = [hold.tile([P, S], U32, name=f"g_words{a}", align_bytes=64) for a in range(PASSES)]
+        g_bytes01 = hold.tile([P, S], U8, name="g_bytes01", align_bytes=64)
+        g_bytes2 = hold.tile([P, S], U8, name="g_bytes2", align_bytes=64)
+        g_bytes = [g_bytes01[4:P, :], g_bytes01[:], g_bytes2[:]]
+        w8 = hold.tile([P, E, 4 * N], U8, name="w8", align_bytes=64)
+        w4 = hold.tile([P, E, 2, 2 * N], U8, name="w4", align_bytes=64)
+        w8_sc = hold.tile([P, E, N], U8, name="w8_sc", align_bytes=64)
+        w4_sc = hold.tile([P, E, 2, N], U8, name="w4_sc", align_bytes=64)
+        gates = hold.tile([P, S], F32, name="gates")
+        bias = hold.tile([P, NB, E], F32, name="bias")
+        resid = hold.tile([P, NB, T], F32, name="resid")
+        placed = [hold.tile([P, T], F32, name=f"placed{c}") for c in range(NB)]
+        result = [hold.tile([P, T], F32, name=f"result{c}") for c in range(NB)]
+        acc = {(e, c): psum.tile([P, C], F32, name=f"acc{e}{c}") for e in range(E) for c in range(NB)}
+        pos = {(e, c): hold.tile([P, C], F32, name=f"pos{e}{c}") for e in range(E) for c in range(NB)}
+        gated = {(e, c): hold.tile([P, C], F32, name=f"gated{e}{c}") for e in range(E) for c in range(NB)}
+        sq = {(e, c): hold.tile([P, C], F32, name=f"sq{e}{c}") for e in range(E) for c in range(NB)}
+
+        nc.vector.memset(w8_sc[:].rearrange("p e n -> p (e n)").bitcast(I32), 0)
+        nc.vector.memset(w4_sc[:].rearrange("p e a n -> p (e a n)").bitcast(I32), 0)
+        for tile in (bytes01, bytes2):
+            nc.gpsimd.memset(tile[:], 0)
+        for c in range(NB):
+            nc.gpsimd.memset(placed[c][:], 0.0)
+
+        def load_x(a, t0, t1):
+            nc.sync.dma_start(x_raw[a][:, :, t0:t1], xT[512 * a : 512 * (a + 1), t0:t1].rearrange("(p j) t -> p j t", j=4))
+
+        def load_w(e):
+            nc.sync.dma_start(w8[:, e, :].bitcast(I32), w8_words[e, 0].rearrange("p n r -> p (n r)").bitcast(I32))
+            nc.sync.dma_start(w4[:, e].bitcast(I32), w4_words[e].rearrange("a p n -> p a n").bitcast(I32))
+
+        def load_scales():
+            for q in range(4):
+                rows = slice(4 * q, 4 * (q + 1))
+                parts = slice(32 * q, 32 * q + 4)
+                nc.sync.dma_start(w8_sc[parts].bitcast(I32), w8_scales[:, 0, rows, :].rearrange("e q n -> q e n").bitcast(I32))
+                nc.sync.dma_start(w4_sc[parts].rearrange("p e a n -> p (e a) n").bitcast(I32), w4_scales.rearrange("e a q n -> q (e a) n")[rows].bitcast(I32))
+
+        def load_bias():
+            nc.sync.dma_start(bias[:], b.rearrange("(c p) e -> p c e", p=P))
+
+        def load_gates():
+            nc.sync.dma_start(gates[:], gate[0:P, :])
+
+        def load_resid(c):
+            nc.sync.dma_start(resid[:, c, :], xr[P * c : P * (c + 1), :])
+
+        def load_offs():
+            nc.sync.dma_start(offsets[:], offs)
+
+        load_x(0, 0, 256)
+        load_x(0, 256, T)
+        load_offs()
+        load_x(1, 0, 256)
+        load_x(1, 256, T)
+        load_scales()
+        load_w(0)
+        load_x(2, 0, 256)
+        load_x(2, 256, 512)
+        load_x(2, 512, T)
+        load_bias()
+        load_gates()
+        load_w(1)
+        for c in range(NB):
+            load_resid(c)
+
+        def group_v(a, t0, t1):
+            nc.vector.tensor_copy(out=x_grp[a][:, t0:t1, :], in_=x_raw[a][:, :, t0:t1].rearrange("p j t -> p t j"))
+
+        def group_s(a, t0, t1):
+            nc.scalar.activation(x_grp[a][:, t0:t1, :], x_raw[a][:, :, t0:t1].rearrange("p j t -> p t j"), ACT.Copy)
+
+        def quant(a, t0, t1):
+            nc.vector.quantize_mx(
+                out=words[a][:, t0:t1].bitcast(FP8X4),
+                scales=bytes_[a][:, t0:t1],
+                in_=x_grp[a][:, t0:t1, :].rearrange("p t j -> p (t j)"),
+            )
+
+        def gather_w(a, e):
+            idx = offsets[:, C // 16 * e : C // 16 * (e + 1)]
+            nc.vector.tensor_copy(g_words[a][:, C * e : C * (e + 1)], words[a][:].indirect(idx))
+
+        def gather_b(a, e):
+            idx = offsets[:, C // 16 * e : C // 16 * (e + 1)]
+            nc.vector.tensor_copy((g_bytes01, g_bytes2)[a // 2][:, C * e : C * (e + 1)], (bytes01, bytes2)[a // 2][:].indirect(idx))
+
+        def multiply(e, c, h, a):
+            cols = slice(C * e + HALF * h, C * e + HALF * (h + 1))
+            if a == 0:
+                codes = w8[:, e, 4 * P * c : 4 * P * (c + 1)].bitcast(FP8X4)
+                scales = w8_sc[:, e, P * c : P * (c + 1)]
+            else:
+                codes = w4[:, e, a - 1, 2 * P * c : 2 * P * (c + 1)].bitcast(FP4X4)
+                scales = w4_sc[:, e, a - 1, P * c : P * (c + 1)]
+            nc.tensor.matmul_mx(
+                out=acc[e, c][:, HALF * h : HALF * (h + 1)],
+                lhsT=codes,
+                lhsT_scale=scales,
+                rhs=g_words[a][:, cols].bitcast(FP8X4),
+                rhs_scale=g_bytes[a][:, cols],
+                start=(a == 0),
+                stop=(a == PASSES - 1),
+            )
+
+        def begin(e, c):
+            multiply(e, c, 0, 0)
+            multiply(e, c, 0, 1)
+
+        def compute(e, c):
+            multiply(e, c, 0, 2)
+            for a in range(PASSES):
+                multiply(e, c, 1, a)
+            nc.scalar.activation(pos[e, c][:], acc[e, c][:], ACT.Relu, bias=bias[:, c, e : e + 1])
+            nc.scalar.activation(sq[e, c][:], pos[e, c][:], ACT.Square)
+            nc.gpsimd.tensor_tensor(gated[e, c][:], sq[e, c][:], gates[:, C * e : C * (e + 1)], ALU.mult)
+
+        def scatter(e, c):
+            idx = offsets[:, C // 16 * e : C // 16 * (e + 1)]
+            nc.vector.tensor_copy(placed[c][:].indirect(idx), gated[e, c][:])
+
+        def finish(engine, c, t0, t1):
+            engine.tensor_tensor(result[c][:, t0:t1], placed[c][:, t0:t1], resid[:, c, t0:t1], ALU.add)
+            nc.sync.dma_start(out[P * c : P * (c + 1), t0:t1], result[c][:, t0:t1])
+
+        group_s(0, 0, 256)
+        group_v(0, 256, 512)
+        group_v(0, 512, T)
+        quant(0, 0, 256)
+        quant(0, 256, 512)
+        quant(0, 512, T)
+        gather_w(0, 0)
+        gather_w(0, 1)
+        group_s(1, 0, 256)
+        group_s(1, 256, 512)
+        group_s(1, 512, T)
+        quant(1, 0, 512)
+        quant(1, 512, T)
+        gather_b(0, 0)
+        gather_w(1, 0)
+        for c in range(NB):
+            begin(0, c)
+        group_s(2, 0, 256)
+        group_s(2, 256, 512)
+        group_v(2, 512, T)
+        quant(2, 0, 256)
+        quant(2, 512, T)
+        quant(2, 256, 512)
+        gather_w(2, 0)
+        gather_b(2, 0)
+        compute(0, 0)
+        gather_b(0, 1)
+        gather_w(1, 1)
+        gather_w(2, 1)
+        gather_b(2, 1)
+        for c in range(NB):
+            begin(1, c)
+
+        order = [(e, c) for c in range(NB) for e in range(E)]
+        for i in range(1, 3):
+            compute(*order[i])
+        for i, (e, c) in enumerate(order):
+            scatter(e, c)
+            if i + 3 < len(order):
+                compute(*order[i + 3])
+            if e == E - 1 and c < NB - 1:
+                finish(nc.gpsimd, c, 0, T)
+        finish(nc.vector, NB - 1, 0, T // 2)
+        finish(nc.vector, NB - 1, T // 2, T)

@@ -1,16 +1,38 @@
 from contextlib import ExitStack
 
 import concourse.mybir as mybir
+from concourse.masks import make_identity
 
 K, T, E, C, N = 1536, 640, 2, 256, 512
 S = E * C
 P = 128
-PASSES = 3
-NB = N // P
-HALF = 128
+PACK = 4
+K_PASS = P * PACK
+PASSES = K // K_PASS
+PASSES8 = 1
+PASSES4 = PASSES - PASSES8
+BLOCKS = N // P
+MOVING = 128
+LIST_ROWS = 16
+PLANE_ROWS = 4
+
+LEAD = 256
+SHARE = 384
+LAST = 512
+FUSED = 2
+AHEAD = 3
 
 FLOPS = 2 * K * N * S
-BYTES = 4 * K * T + 4 * N * T + E * (K // 3) * N + E * (2 * K // 3) * N // 2 + E * (K // 32) * N + 4 * N * E + 4 * S + 2 * P * (S // 16) + 4 * N * T
+BYTES = (
+    4 * K * T
+    + 2 * 4 * N * T
+    + E * K_PASS * PASSES8 * N
+    + E * K_PASS * PASSES4 * N // 2
+    + E * (K // 32) * N
+    + 4 * N * E
+    + 4 * S
+    + 2 * S * 8
+)
 
 F32 = mybir.dt.float32
 BF16 = mybir.dt.bfloat16
@@ -31,180 +53,204 @@ def tile_moe_res_lin_relu2_kernel(tc, xT, xr, w8_words, w8_scales, w4_words, w4_
         hold = ctx.enter_context(tc.tile_pool(name="hold", bufs=1))
         psum = ctx.enter_context(tc.psum_pool(name="psum", bufs=1))
 
-        offsets = lists.tile([P, S // 16], U16, name="offsets")
-        x_raw = [hold.tile([P, 4, T], F32, name=f"x_raw{a}", align_bytes=64) for a in range(PASSES)]
-        x_grp = [hold.tile([P, T, 4], BF16, name=f"x_grp{a}", align_bytes=64) for a in range(PASSES)]
+        offsets = lists.tile([P, S // LIST_ROWS], U16, name="offsets")
+        raw = [hold.tile([P, PACK, T], F32, name=f"raw{a}", align_bytes=64) for a in range(PASSES)]
+        grouped = [hold.tile([P, T, PACK], BF16, name=f"grouped{a}", align_bytes=64) for a in range(PASSES)]
         words = [hold.tile([P, T], U32, name=f"words{a}", align_bytes=64) for a in range(PASSES)]
-        bytes01 = hold.tile([P, T], U8, name="scale_bytes01", align_bytes=64)
-        bytes2 = hold.tile([P, T], U8, name="scale_bytes2", align_bytes=64)
-        bytes_ = [bytes01[4:P, :], bytes01[:], bytes2[:]]
-        g_words = [hold.tile([P, S], U32, name=f"g_words{a}", align_bytes=64) for a in range(PASSES)]
-        g_bytes01 = hold.tile([P, S], U8, name="g_bytes01", align_bytes=64)
-        g_bytes2 = hold.tile([P, S], U8, name="g_bytes2", align_bytes=64)
-        g_bytes = [g_bytes01[4:P, :], g_bytes01[:], g_bytes2[:]]
-        w8 = hold.tile([P, E, 4 * N], U8, name="w8", align_bytes=64)
-        w4 = hold.tile([P, E, 2, 2 * N], U8, name="w4", align_bytes=64)
-        w8_sc = hold.tile([P, E, N], U8, name="w8_sc", align_bytes=64)
-        w4_sc = hold.tile([P, E, 2, N], U8, name="w4_sc", align_bytes=64)
+        bytes01 = hold.tile([P, T], U8, name="bytes01", align_bytes=64)
+        bytes2 = hold.tile([P, T], U8, name="bytes2", align_bytes=64)
+        slot_words = [hold.tile([P, S], U32, name=f"slot_words{a}", align_bytes=64) for a in range(PASSES)]
+        slot_bytes01 = hold.tile([P, S], U8, name="slot_bytes01", align_bytes=64)
+        slot_bytes2 = hold.tile([P, S], U8, name="slot_bytes2", align_bytes=64)
+        w8 = hold.tile([P, E, PACK * N], U8, name="w8", align_bytes=64)
+        w4 = hold.tile([P, E, PASSES4, PACK * N // 2], U8, name="w4", align_bytes=64)
+        w8_bytes = hold.tile([P, E, N], U8, name="w8_bytes", align_bytes=64)
+        w4_bytes = hold.tile([P, E, PASSES4, N], U8, name="w4_bytes", align_bytes=64)
         gates = hold.tile([P, S], F32, name="gates")
-        bias = hold.tile([P, NB, E], F32, name="bias")
-        resid = hold.tile([P, NB, T], F32, name="resid")
-        placed = [hold.tile([P, T], F32, name=f"placed{c}") for c in range(NB)]
-        result = [hold.tile([P, T], F32, name=f"result{c}") for c in range(NB)]
-        acc = {(e, c): psum.tile([P, C], F32, name=f"acc{e}{c}") for e in range(E) for c in range(NB)}
-        pos = {(e, c): hold.tile([P, C], F32, name=f"pos{e}{c}") for e in range(E) for c in range(NB)}
-        gated = {(e, c): hold.tile([P, C], F32, name=f"gated{e}{c}") for e in range(E) for c in range(NB)}
-        sq = {(e, c): hold.tile([P, C], F32, name=f"sq{e}{c}") for e in range(E) for c in range(NB)}
+        identity = hold.tile([P, P], F32, name="identity", align_bytes=64)
+        b_rows = hold.tile([P, P, E], F32, name="b_rows", align_bytes=64)
+        bias = hold.tile([P, E, BLOCKS], F32, name="bias")
+        residual = hold.tile([P, BLOCKS, T], F32, name="residual")
+        placed = [hold.tile([P, T], F32, name=f"placed{n}") for n in range(BLOCKS)]
+        result = [hold.tile([P, T], F32, name=f"result{n}") for n in range(BLOCKS)]
 
-        nc.vector.memset(w8_sc[:].rearrange("p e n -> p (e n)").bitcast(I32), 0)
-        nc.vector.memset(w4_sc[:].rearrange("p e a n -> p (e a n)").bitcast(I32), 0)
+        order = [(e, n) for e in range(E) for n in range(BLOCKS)]
+        sums = {(e, n): psum.tile([P, C], F32, name=f"sums{e}{n}") for e, n in order}
+        positive = {(e, n): hold.tile([P, C], F32, name=f"positive{e}{n}") for e, n in order}
+        squared = {(e, n): hold.tile([P, C], F32, name=f"squared{e}{n}") for e, n in order}
+        weighted = {(e, n): hold.tile([P, C], F32, name=f"weighted{e}{n}") for e, n in order}
+
+        plane = [bytes01[PLANE_ROWS:P, :], bytes01[:], bytes2[:]]
+        slot_plane = [slot_bytes01[PLANE_ROWS:P, :], slot_bytes01[:], slot_bytes2[:]]
+
+        nc.vector.memset(w4_bytes[:].rearrange("p e a n -> p (e a n)").bitcast(I32), 0)
+        nc.vector.memset(w8_bytes[:].rearrange("p e n -> p (e n)").bitcast(I32), 0)
+        nc.vector.memset(b_rows[:], 0.0)
         for tile in (bytes01, bytes2):
-            nc.gpsimd.memset(tile[:], 0)
-        for c in range(NB):
-            nc.gpsimd.memset(placed[c][:], 0.0)
+            nc.vector.memset(tile[:].bitcast(I32), 0)
+        for n in range(BLOCKS):
+            nc.vector.memset(placed[n][:], 0.0)
+        make_identity(nc, identity[:])
 
-        def load_x(a, t0, t1):
-            nc.sync.dma_start(x_raw[a][:, :, t0:t1], xT[512 * a : 512 * (a + 1), t0:t1].rearrange("(p j) t -> p j t", j=4))
-
-        def load_w(e):
-            nc.sync.dma_start(w8[:, e, :].bitcast(I32), w8_words[e, 0].rearrange("p n r -> p (n r)").bitcast(I32))
-            nc.sync.dma_start(w4[:, e].bitcast(I32), w4_words[e].rearrange("a p n -> p a n").bitcast(I32))
-
-        def load_scales():
-            for q in range(4):
-                rows = slice(4 * q, 4 * (q + 1))
-                parts = slice(32 * q, 32 * q + 4)
-                nc.sync.dma_start(w8_sc[parts].bitcast(I32), w8_scales[:, 0, rows, :].rearrange("e q n -> q e n").bitcast(I32))
-                nc.sync.dma_start(w4_sc[parts].rearrange("p e a n -> p (e a) n").bitcast(I32), w4_scales.rearrange("e a q n -> q (e a) n")[rows].bitcast(I32))
-
-        def load_bias():
-            nc.sync.dma_start(bias[:], b.rearrange("(c p) e -> p c e", p=P))
-
-        def load_gates():
-            nc.sync.dma_start(gates[:], gate[0:P, :])
-
-        def load_resid(c):
-            nc.sync.dma_start(resid[:, c, :], xr[P * c : P * (c + 1), :])
-
-        def load_offs():
-            nc.sync.dma_start(offsets[:], offs)
-
-        load_x(0, 0, 256)
-        load_x(0, 256, T)
-        load_offs()
-        load_x(1, 0, 256)
-        load_x(1, 256, T)
-        load_scales()
-        load_w(0)
-        load_x(2, 0, 256)
-        load_x(2, 256, 512)
-        load_x(2, 512, T)
-        load_bias()
-        load_gates()
-        load_w(1)
-        for c in range(NB):
-            load_resid(c)
-
-        def group_v(a, t0, t1):
-            nc.vector.tensor_copy(out=x_grp[a][:, t0:t1, :], in_=x_raw[a][:, :, t0:t1].rearrange("p j t -> p t j"))
-
-        def group_s(a, t0, t1):
-            nc.scalar.activation(x_grp[a][:, t0:t1, :], x_raw[a][:, :, t0:t1].rearrange("p j t -> p t j"), ACT.Copy)
-
-        def quant(a, t0, t1):
-            nc.vector.quantize_mx(
-                out=words[a][:, t0:t1].bitcast(FP8X4),
-                scales=bytes_[a][:, t0:t1],
-                in_=x_grp[a][:, t0:t1, :].rearrange("p t j -> p (t j)"),
+        for g in range(P // 32):
+            nc.gpsimd.dma_start(
+                w4_bytes[32 * g : 32 * g + PLANE_ROWS].rearrange("p e a n -> p (e a) n").bitcast(I32),
+                w4_scales.rearrange("e a q n -> q (e a) n")[PLANE_ROWS * g : PLANE_ROWS * (g + 1)].bitcast(I32),
             )
 
-        def gather_w(a, e):
-            idx = offsets[:, C // 16 * e : C // 16 * (e + 1)]
-            nc.vector.tensor_copy(g_words[a][:, C * e : C * (e + 1)], words[a][:].indirect(idx))
+        def load_tokens(a, t0, t1):
+            rows = xT[K_PASS * a : K_PASS * (a + 1), t0:t1]
+            nc.sync.dma_start(raw[a][:, :, t0:t1], rows.rearrange("(p j) t -> p j t", j=PACK))
 
-        def gather_b(a, e):
-            idx = offsets[:, C // 16 * e : C // 16 * (e + 1)]
-            nc.vector.tensor_copy((g_bytes01, g_bytes2)[a // 2][:, C * e : C * (e + 1)], (bytes01, bytes2)[a // 2][:].indirect(idx))
+        def load_weights(e):
+            nc.sync.dma_start(w8[:, e, :].bitcast(I32), w8_words[e, 0].rearrange("p n r -> p (n r)").bitcast(I32))
+            nc.sync.dma_start(w4[:, e].bitcast(I32), w4_words[e].rearrange("a p m -> p a m").bitcast(I32))
 
-        def multiply(e, c, h, a):
-            cols = slice(C * e + HALF * h, C * e + HALF * (h + 1))
-            if a == 0:
-                codes = w8[:, e, 4 * P * c : 4 * P * (c + 1)].bitcast(FP8X4)
-                scales = w8_sc[:, e, P * c : P * (c + 1)]
+        load_tokens(0, 0, LEAD)
+        load_tokens(0, LEAD, T)
+        nc.sync.dma_start(offsets[:], offs)
+        nc.sync.dma_start(b_rows[0:BLOCKS], b.rearrange("(n p) e -> n p e", p=P))
+        load_tokens(1, 0, LEAD)
+        load_tokens(1, LEAD, T)
+        load_tokens(2, 0, LEAD)
+        load_tokens(2, LEAD, LAST)
+        load_tokens(2, LAST, T)
+        for g in range(P // 32):
+            nc.sync.dma_start(
+                w8_bytes[32 * g : 32 * g + PLANE_ROWS].bitcast(I32),
+                w8_scales[:, 0, PLANE_ROWS * g : PLANE_ROWS * (g + 1), :].rearrange("e q n -> q e n").bitcast(I32),
+            )
+        load_weights(0)
+        nc.sync.dma_start(gates[:], gate[0:P, :])
+        load_weights(1)
+        for n in range(BLOCKS):
+            nc.sync.dma_start(residual[:, n, :], xr[P * n : P * (n + 1), :])
+
+        def interleaved(a, t0, t1):
+            return grouped[a][:, t0:t1, :], raw[a][:, :, t0:t1].rearrange("p j t -> p t j")
+
+        def interleave_on_scalar(a, t0, t1):
+            to, source = interleaved(a, t0, t1)
+            nc.scalar.activation(to, source, ACT.Copy)
+
+        def interleave_on_vector(a, t0, t1):
+            to, source = interleaved(a, t0, t1)
+            nc.vector.tensor_copy(to, source)
+
+        def quantise(a, t0, t1):
+            nc.vector.quantize_mx(
+                out=words[a][:, t0:t1].bitcast(FP8X4),
+                scales=plane[a][:, t0:t1],
+                in_=grouped[a][:, t0:t1, :].rearrange("p t j -> p (t j)"),
+            )
+
+        def expert_slots(e):
+            return slice(C * e, C * (e + 1))
+
+        def expert_offsets(e):
+            return offsets[:, C // LIST_ROWS * e : C // LIST_ROWS * (e + 1)]
+
+        def gather_words(a, e):
+            nc.vector.tensor_copy(slot_words[a][:, expert_slots(e)], words[a][:].indirect(expert_offsets(e)))
+
+        def gather_bytes01(e):
+            nc.vector.tensor_copy(slot_bytes01[:, expert_slots(e)], bytes01[:].indirect(expert_offsets(e)))
+
+        def gather_bytes2(e):
+            nc.vector.tensor_copy(slot_bytes2[:, expert_slots(e)], bytes2[:].indirect(expert_offsets(e)))
+
+        def multiply(e, n, h, a):
+            if a < PASSES8:
+                codes = w8[:, e, PACK * P * n : PACK * P * (n + 1)].bitcast(FP8X4)
+                scales = w8_bytes[:, e, P * n : P * (n + 1)]
             else:
-                codes = w4[:, e, a - 1, 2 * P * c : 2 * P * (c + 1)].bitcast(FP4X4)
-                scales = w4_sc[:, e, a - 1, P * c : P * (c + 1)]
+                codes = w4[:, e, a - PASSES8, PACK * P * n // 2 : PACK * P * (n + 1) // 2].bitcast(FP4X4)
+                scales = w4_bytes[:, e, a - PASSES8, P * n : P * (n + 1)]
+            slots = slice(C * e + MOVING * h, C * e + MOVING * (h + 1))
             nc.tensor.matmul_mx(
-                out=acc[e, c][:, HALF * h : HALF * (h + 1)],
+                out=sums[e, n][:, MOVING * h : MOVING * (h + 1)],
                 lhsT=codes,
                 lhsT_scale=scales,
-                rhs=g_words[a][:, cols].bitcast(FP8X4),
-                rhs_scale=g_bytes[a][:, cols],
+                rhs=slot_words[a][:, slots].bitcast(FP8X4),
+                rhs_scale=slot_plane[a][:, slots],
                 start=(a == 0),
                 stop=(a == PASSES - 1),
             )
 
-        def begin(e, c):
-            multiply(e, c, 0, 0)
-            multiply(e, c, 0, 1)
+        def begin(e, n):
+            for a in range(PASSES - 1):
+                multiply(e, n, 0, a)
 
-        def compute(e, c):
-            multiply(e, c, 0, 2)
+        def compute(i):
+            e, n = order[i]
+            if e > 0:
+                begin(e, n)
+            multiply(e, n, 0, PASSES - 1)
             for a in range(PASSES):
-                multiply(e, c, 1, a)
-            nc.scalar.activation(pos[e, c][:], acc[e, c][:], ACT.Relu, bias=bias[:, c, e : e + 1])
-            nc.scalar.activation(sq[e, c][:], pos[e, c][:], ACT.Square)
-            nc.gpsimd.tensor_tensor(gated[e, c][:], sq[e, c][:], gates[:, C * e : C * (e + 1)], ALU.mult)
+                multiply(e, n, 1, a)
+            nc.scalar.activation(positive[e, n][:], sums[e, n][:], ACT.Relu, bias=bias[:, e, n : n + 1])
+            nc.scalar.activation(squared[e, n][:], positive[e, n][:], ACT.Square)
+            if i >= FUSED:
+                nc.gpsimd.tensor_tensor(weighted[e, n][:], squared[e, n][:], gates[:, expert_slots(e)], ALU.mult)
 
-        def scatter(e, c):
-            idx = offsets[:, C // 16 * e : C // 16 * (e + 1)]
-            nc.vector.tensor_copy(placed[c][:].indirect(idx), gated[e, c][:])
+        def scatter(i):
+            e, n = order[i]
+            columns = placed[n][:].indirect(expert_offsets(e))
+            if i >= FUSED:
+                nc.vector.tensor_copy(columns, weighted[e, n][:])
+            else:
+                nc.vector.tensor_tensor(columns, squared[e, n][:], gates[:, expert_slots(e)], ALU.mult)
 
-        def finish(engine, c, t0, t1):
-            engine.tensor_tensor(result[c][:, t0:t1], placed[c][:, t0:t1], resid[:, c, t0:t1], ALU.add)
-            nc.sync.dma_start(out[P * c : P * (c + 1), t0:t1], result[c][:, t0:t1])
+        def finish(engine, n, t0, t1):
+            engine.tensor_tensor(result[n][:, t0:t1], placed[n][:, t0:t1], residual[:, n, t0:t1], ALU.add)
+            nc.sync.dma_start(out[P * n : P * (n + 1), t0:t1], result[n][:, t0:t1])
 
-        group_s(0, 0, 256)
-        group_v(0, 256, 512)
-        group_v(0, 512, T)
-        quant(0, 0, 256)
-        quant(0, 256, 512)
-        quant(0, 512, T)
-        gather_w(0, 0)
-        gather_w(0, 1)
-        group_s(1, 0, 256)
-        group_s(1, 256, 512)
-        group_s(1, 512, T)
-        quant(1, 0, 512)
-        quant(1, 512, T)
-        gather_b(0, 0)
-        gather_w(1, 0)
-        for c in range(NB):
-            begin(0, c)
-        group_s(2, 0, 256)
-        group_s(2, 256, 512)
-        group_v(2, 512, T)
-        quant(2, 0, 256)
-        quant(2, 512, T)
-        quant(2, 256, 512)
-        gather_w(2, 0)
-        gather_b(2, 0)
-        compute(0, 0)
-        gather_b(0, 1)
-        gather_w(1, 1)
-        gather_w(2, 1)
-        gather_b(2, 1)
-        for c in range(NB):
-            begin(1, c)
+        interleave_on_scalar(0, 0, LEAD)
+        interleave_on_scalar(0, LEAD, SHARE)
+        interleave_on_vector(0, SHARE, T)
+        for t0, t1 in ((0, LEAD), (LEAD, SHARE), (SHARE, T)):
+            quantise(0, t0, t1)
+        for e in range(E):
+            gather_words(0, e)
 
-        order = [(e, c) for c in range(NB) for e in range(E)]
-        for i in range(1, 3):
-            compute(*order[i])
-        for i, (e, c) in enumerate(order):
-            scatter(e, c)
-            if i + 3 < len(order):
-                compute(*order[i + 3])
-            if e == E - 1 and c < NB - 1:
-                finish(nc.gpsimd, c, 0, T)
-        finish(nc.vector, NB - 1, 0, T // 2)
-        finish(nc.vector, NB - 1, T // 2, T)
+        turned = sums[E - 1, BLOCKS - 1][:].rearrange("p (e m) -> p e m", e=E)
+        for e in range(E):
+            nc.tensor.transpose(turned[:, e, :], b_rows[:, :, e], identity[:])
+
+        interleave_on_scalar(1, 0, LEAD)
+        interleave_on_scalar(1, LEAD, SHARE)
+        nc.scalar.activation(bias[:], turned[:, :, 0:BLOCKS], ACT.Copy)
+        interleave_on_vector(1, SHARE, T)
+        for t0, t1 in ((0, LEAD), (LEAD, SHARE), (SHARE, T)):
+            quantise(1, t0, t1)
+        gather_bytes01(0)
+        gather_words(1, 0)
+        for n in range(BLOCKS):
+            begin(0, n)
+
+        interleave_on_scalar(2, 0, LEAD)
+        quantise(2, 0, LEAD)
+        interleave_on_scalar(2, LEAD, SHARE)
+        interleave_on_vector(2, SHARE, LAST)
+        interleave_on_vector(2, LAST, T)
+        quantise(2, LEAD, LAST)
+        quantise(2, LAST, T)
+        gather_words(2, 0)
+        gather_bytes2(0)
+        compute(0)
+        gather_bytes01(1)
+        gather_words(1, 1)
+        compute(1)
+        gather_words(2, 1)
+        gather_bytes2(1)
+        compute(2)
+
+        for i in range(len(order)):
+            scatter(i)
+            if i + AHEAD < len(order):
+                compute(i + AHEAD)
+            e, n = order[i]
+            if e == E - 1 and n < BLOCKS - 1:
+                finish(nc.gpsimd, n, 0, T)
+        finish(nc.vector, BLOCKS - 1, 0, T // 2)
+        finish(nc.vector, BLOCKS - 1, T // 2, T)

from contextlib import ExitStack

import concourse.mybir as mybir
from concourse.masks import make_identity

K, T, E, C, N = 1536, 640, 2, 256, 512
S = E * C
P = 128
PACK = 4
K_PASS = P * PACK
PASSES = K // K_PASS
PASSES8 = 1
PASSES4 = PASSES - PASSES8
BLOCKS = N // P
MOVING = 128
LIST_ROWS = 16
PLANE_ROWS = 4

LEAD = 256
SHARE = 384
LAST = 512
FUSED = 2
AHEAD = 3

FLOPS = 2 * K * N * S
BYTES = (
    4 * K * T
    + 2 * 4 * N * T
    + E * K_PASS * PASSES8 * N
    + E * K_PASS * PASSES4 * N // 2
    + E * (K // 32) * N
    + 4 * N * E
    + 4 * S
    + 2 * S * 8
)

F32 = mybir.dt.float32
BF16 = mybir.dt.bfloat16
I32 = mybir.dt.int32
U32 = mybir.dt.uint32
U16 = mybir.dt.uint16
U8 = mybir.dt.uint8
FP8X4 = mybir.dt.float8_e4m3fn_x4
FP4X4 = mybir.dt.float4_e2m1fn_x4
ACT = mybir.ActivationFunctionType
ALU = mybir.AluOpType


def tile_moe_res_lin_relu2_kernel(tc, xT, xr, w8_words, w8_scales, w4_words, w4_scales, b, gate, offs, out):
    nc = tc.nc
    with ExitStack() as ctx:
        lists = ctx.enter_context(tc.tile_pool(name="lists", bufs=1))
        hold = ctx.enter_context(tc.tile_pool(name="hold", bufs=1))
        psum = ctx.enter_context(tc.psum_pool(name="psum", bufs=1))

        offsets = lists.tile([P, S // LIST_ROWS], U16, name="offsets")
        raw = [hold.tile([P, PACK, T], F32, name=f"raw{a}", align_bytes=64) for a in range(PASSES)]
        grouped = [hold.tile([P, T, PACK], BF16, name=f"grouped{a}", align_bytes=64) for a in range(PASSES)]
        words = [hold.tile([P, T], U32, name=f"words{a}", align_bytes=64) for a in range(PASSES)]
        bytes01 = hold.tile([P, T], U8, name="bytes01", align_bytes=64)
        bytes2 = hold.tile([P, T], U8, name="bytes2", align_bytes=64)
        slot_words = [hold.tile([P, S], U32, name=f"slot_words{a}", align_bytes=64) for a in range(PASSES)]
        slot_bytes01 = hold.tile([P, S], U8, name="slot_bytes01", align_bytes=64)
        slot_bytes2 = hold.tile([P, S], U8, name="slot_bytes2", align_bytes=64)
        w8 = hold.tile([P, E, PACK * N], U8, name="w8", align_bytes=64)
        w4 = hold.tile([P, E, PASSES4, PACK * N // 2], U8, name="w4", align_bytes=64)
        w8_bytes = hold.tile([P, E, N], U8, name="w8_bytes", align_bytes=64)
        w4_bytes = hold.tile([P, E, PASSES4, N], U8, name="w4_bytes", align_bytes=64)
        gates = hold.tile([P, S], F32, name="gates")
        identity = hold.tile([P, P], F32, name="identity", align_bytes=64)
        b_rows = hold.tile([P, P, E], F32, name="b_rows", align_bytes=64)
        bias = hold.tile([P, E, BLOCKS], F32, name="bias")
        residual = hold.tile([P, BLOCKS, T], F32, name="residual")
        placed = [hold.tile([P, T], F32, name=f"placed{n}") for n in range(BLOCKS)]
        result = [hold.tile([P, T], F32, name=f"result{n}") for n in range(BLOCKS)]

        order = [(e, n) for e in range(E) for n in range(BLOCKS)]
        sums = {(e, n): psum.tile([P, C], F32, name=f"sums{e}{n}") for e, n in order}
        positive = {(e, n): hold.tile([P, C], F32, name=f"positive{e}{n}") for e, n in order}
        squared = {(e, n): hold.tile([P, C], F32, name=f"squared{e}{n}") for e, n in order}
        weighted = {(e, n): hold.tile([P, C], F32, name=f"weighted{e}{n}") for e, n in order}

        plane = [bytes01[PLANE_ROWS:P, :], bytes01[:], bytes2[:]]
        slot_plane = [slot_bytes01[PLANE_ROWS:P, :], slot_bytes01[:], slot_bytes2[:]]

        nc.vector.memset(w4_bytes[:].rearrange("p e a n -> p (e a n)").bitcast(I32), 0)
        nc.vector.memset(w8_bytes[:].rearrange("p e n -> p (e n)").bitcast(I32), 0)
        nc.vector.memset(b_rows[:], 0.0)
        for tile in (bytes01, bytes2):
            nc.vector.memset(tile[:].bitcast(I32), 0)
        for n in range(BLOCKS):
            nc.vector.memset(placed[n][:], 0.0)
        make_identity(nc, identity[:])

        for g in range(P // 32):
            nc.gpsimd.dma_start(
                w4_bytes[32 * g : 32 * g + PLANE_ROWS].rearrange("p e a n -> p (e a) n").bitcast(I32),
                w4_scales.rearrange("e a q n -> q (e a) n")[PLANE_ROWS * g : PLANE_ROWS * (g + 1)].bitcast(I32),
            )

        def load_tokens(a, t0, t1):
            rows = xT[K_PASS * a : K_PASS * (a + 1), t0:t1]
            nc.sync.dma_start(raw[a][:, :, t0:t1], rows.rearrange("(p j) t -> p j t", j=PACK))

        def load_weights(e):
            nc.sync.dma_start(w8[:, e, :].bitcast(I32), w8_words[e, 0].rearrange("p n r -> p (n r)").bitcast(I32))
            nc.sync.dma_start(w4[:, e].bitcast(I32), w4_words[e].rearrange("a p m -> p a m").bitcast(I32))

        load_tokens(0, 0, LEAD)
        load_tokens(0, LEAD, T)
        nc.sync.dma_start(offsets[:], offs)
        nc.sync.dma_start(b_rows[0:BLOCKS], b.rearrange("(n p) e -> n p e", p=P))
        load_tokens(1, 0, LEAD)
        load_tokens(1, LEAD, T)
        load_tokens(2, 0, LEAD)
        load_tokens(2, LEAD, LAST)
        load_tokens(2, LAST, T)
        for g in range(P // 32):
            nc.sync.dma_start(
                w8_bytes[32 * g : 32 * g + PLANE_ROWS].bitcast(I32),
                w8_scales[:, 0, PLANE_ROWS * g : PLANE_ROWS * (g + 1), :].rearrange("e q n -> q e n").bitcast(I32),
            )
        load_weights(0)
        nc.sync.dma_start(gates[:], gate[0:P, :])
        load_weights(1)
        for n in range(BLOCKS):
            nc.sync.dma_start(residual[:, n, :], xr[P * n : P * (n + 1), :])

        def interleaved(a, t0, t1):
            return grouped[a][:, t0:t1, :], raw[a][:, :, t0:t1].rearrange("p j t -> p t j")

        def interleave_on_scalar(a, t0, t1):
            to, source = interleaved(a, t0, t1)
            nc.scalar.activation(to, source, ACT.Copy)

        def interleave_on_vector(a, t0, t1):
            to, source = interleaved(a, t0, t1)
            nc.vector.tensor_copy(to, source)

        def quantise(a, t0, t1):
            nc.vector.quantize_mx(
                out=words[a][:, t0:t1].bitcast(FP8X4),
                scales=plane[a][:, t0:t1],
                in_=grouped[a][:, t0:t1, :].rearrange("p t j -> p (t j)"),
            )

        def expert_slots(e):
            return slice(C * e, C * (e + 1))

        def expert_offsets(e):
            return offsets[:, C // LIST_ROWS * e : C // LIST_ROWS * (e + 1)]

        def gather_words(a, e):
            nc.vector.tensor_copy(slot_words[a][:, expert_slots(e)], words[a][:].indirect(expert_offsets(e)))

        def gather_bytes01(e):
            nc.vector.tensor_copy(slot_bytes01[:, expert_slots(e)], bytes01[:].indirect(expert_offsets(e)))

        def gather_bytes2(e):
            nc.vector.tensor_copy(slot_bytes2[:, expert_slots(e)], bytes2[:].indirect(expert_offsets(e)))

        def multiply(e, n, h, a):
            if a < PASSES8:
                codes = w8[:, e, PACK * P * n : PACK * P * (n + 1)].bitcast(FP8X4)
                scales = w8_bytes[:, e, P * n : P * (n + 1)]
            else:
                codes = w4[:, e, a - PASSES8, PACK * P * n // 2 : PACK * P * (n + 1) // 2].bitcast(FP4X4)
                scales = w4_bytes[:, e, a - PASSES8, P * n : P * (n + 1)]
            slots = slice(C * e + MOVING * h, C * e + MOVING * (h + 1))
            nc.tensor.matmul_mx(
                out=sums[e, n][:, MOVING * h : MOVING * (h + 1)],
                lhsT=codes,
                lhsT_scale=scales,
                rhs=slot_words[a][:, slots].bitcast(FP8X4),
                rhs_scale=slot_plane[a][:, slots],
                start=(a == 0),
                stop=(a == PASSES - 1),
            )

        def begin(e, n):
            for a in range(PASSES - 1):
                multiply(e, n, 0, a)

        def compute(i):
            e, n = order[i]
            if e > 0:
                begin(e, n)
            multiply(e, n, 0, PASSES - 1)
            for a in range(PASSES):
                multiply(e, n, 1, a)
            nc.scalar.activation(positive[e, n][:], sums[e, n][:], ACT.Relu, bias=bias[:, e, n : n + 1])
            nc.scalar.activation(squared[e, n][:], positive[e, n][:], ACT.Square)
            if i >= FUSED:
                nc.gpsimd.tensor_tensor(weighted[e, n][:], squared[e, n][:], gates[:, expert_slots(e)], ALU.mult)

        def scatter(i):
            e, n = order[i]
            columns = placed[n][:].indirect(expert_offsets(e))
            if i >= FUSED:
                nc.vector.tensor_copy(columns, weighted[e, n][:])
            else:
                nc.vector.tensor_tensor(columns, squared[e, n][:], gates[:, expert_slots(e)], ALU.mult)

        def finish(engine, n, t0, t1):
            engine.tensor_tensor(result[n][:, t0:t1], placed[n][:, t0:t1], residual[:, n, t0:t1], ALU.add)
            nc.sync.dma_start(out[P * n : P * (n + 1), t0:t1], result[n][:, t0:t1])

        interleave_on_scalar(0, 0, LEAD)
        interleave_on_scalar(0, LEAD, SHARE)
        interleave_on_vector(0, SHARE, T)
        for t0, t1 in ((0, LEAD), (LEAD, SHARE), (SHARE, T)):
            quantise(0, t0, t1)
        for e in range(E):
            gather_words(0, e)

        turned = sums[E - 1, BLOCKS - 1][:].rearrange("p (e m) -> p e m", e=E)
        for e in range(E):
            nc.tensor.transpose(turned[:, e, :], b_rows[:, :, e], identity[:])

        interleave_on_scalar(1, 0, LEAD)
        interleave_on_scalar(1, LEAD, SHARE)
        nc.scalar.activation(bias[:], turned[:, :, 0:BLOCKS], ACT.Copy)
        interleave_on_vector(1, SHARE, T)
        for t0, t1 in ((0, LEAD), (LEAD, SHARE), (SHARE, T)):
            quantise(1, t0, t1)
        gather_bytes01(0)
        gather_words(1, 0)
        for n in range(BLOCKS):
            begin(0, n)

        interleave_on_scalar(2, 0, LEAD)
        quantise(2, 0, LEAD)
        interleave_on_scalar(2, LEAD, SHARE)
        interleave_on_vector(2, SHARE, LAST)
        interleave_on_vector(2, LAST, T)
        quantise(2, LEAD, LAST)
        quantise(2, LAST, T)
        gather_words(2, 0)
        gather_bytes2(0)
        compute(0)
        gather_bytes01(1)
        gather_words(1, 1)
        compute(1)
        gather_words(2, 1)
        gather_bytes2(1)
        compute(2)

        for i in range(len(order)):
            scatter(i)
            if i + AHEAD < len(order):
                compute(i + AHEAD)
            e, n = order[i]
            if e == E - 1 and n < BLOCKS - 1:
                finish(nc.gpsimd, n, 0, T)
        finish(nc.vector, BLOCKS - 1, 0, T // 2)
        finish(nc.vector, BLOCKS - 1, T // 2, T)
